import numpy as np
import ml_dtypes


def mxq(x, axis, fmt="e4m3"):
    dtype, down = {"e4m3": (ml_dtypes.float8_e4m3fn, 7), "e5m2": (ml_dtypes.float8_e5m2, 14)}[fmt]
    v = np.moveaxis(np.asarray(x, np.float32).astype(ml_dtypes.bfloat16).astype(np.float64), axis, -1)
    blocks = v.reshape(v.shape[:-1] + (-1, 32))
    amax = np.abs(blocks).max(-1, keepdims=True)
    byte = np.maximum(np.where(amax > 0, np.frexp(amax)[1] - 1 + 127, 0) - down, 1)
    scale = np.exp2(byte - 127.0)
    codes = (blocks / scale).astype(np.float32).astype(dtype).astype(np.float64)
    return np.moveaxis((codes * scale).reshape(v.shape), -1, axis)


WIDE = False


def mx_kscale(k):
    if not WIDE:
        return np.ones(k)
    levels = np.array([10, -10, 5, -5, 0])
    if k % 512:
        return np.exp2(np.random.permutation(np.resize(levels, k // 32))).repeat(32)
    a = np.empty((k // 512, 16))
    for p in range(k // 512):
        a[p, :8] = np.random.permutation(np.resize(levels, 8))
        for g in range(8):
            far = levels[np.abs(levels - a[p, g]) >= 10]
            a[p, g + 8] = far[np.random.randint(len(far))]
    return np.exp2(a.ravel()).repeat(32)


def f64(x):
    return np.asarray(x).astype(np.float64)


def striped(idx):
    return np.tile(idx.reshape(-1, 16).T, (8, 1)).astype(np.uint16)


def unstriped(offs):
    return offs[:16].T.reshape(-1).astype(np.int64)


def pack_weight(w):
    k, n = w.shape
    w = f64(np.asarray(w, np.float32).astype(ml_dtypes.bfloat16)).reshape(k // 32, 32, n)
    amax = np.abs(w).max(1)
    byte = np.clip(np.where(amax > 0, np.frexp(amax)[1] - 1 + 127 - 7, 1), 1, 254)
    scaled = (w * np.exp2(127.0 - byte)[:, None, :]).reshape(k, n).astype(np.float32)
    words = np.ascontiguousarray(scaled.reshape(k // 512, 128, 4, n).transpose(0, 1, 3, 2)).astype(ml_dtypes.float8_e4m3fn).view(np.uint8)
    return words, np.ascontiguousarray(byte.astype(np.uint8).reshape(k // 512, 16, n))


def unpack_weight(words, scales):
    g, p, n, _ = words.shape
    vals = np.ascontiguousarray(words).view(ml_dtypes.float8_e4m3fn).astype(np.float64) * np.repeat(np.exp2(scales.astype(np.float64) - 127.0), 8, axis=1)[..., None]
    return vals.transpose(0, 1, 3, 2).reshape(g * 512, n)


E2M1 = np.array([0.0, 0.5, 1.0, 1.5, 2.0, 3.0, 4.0, 6.0, -0.0, -0.5, -1.0, -1.5, -2.0, -3.0, -4.0, -6.0])


def pack_fp4(w):
    k, n = w.shape
    w = f64(np.asarray(w, np.float32).astype(ml_dtypes.bfloat16)).reshape(k // 32, 32, n)
    amax = np.abs(w).max(1)
    mant, ex = np.frexp(amax / 6.0)
    byte = np.clip(np.where(amax > 0, np.where(mant > 0.5, ex, ex - 1) + 127, 1), 1, 254)
    scaled = (w * np.exp2(127.0 - byte)[:, None, :]).reshape(k, n).astype(np.float32)
    c = np.ascontiguousarray(scaled.reshape(k // 512, 128, 4, n).transpose(0, 1, 3, 2)).astype(ml_dtypes.float4_e2m1fn).view(np.uint8) & 0xF
    words = (c[..., 0::2] | (c[..., 1::2] << 4)).reshape(k // 512, 128, 2 * n)
    return np.ascontiguousarray(words), np.ascontiguousarray(byte.astype(np.uint8).reshape(k // 512, 16, n))


def unpack_fp4(words, scales):
    g, _, n = scales.shape
    words = np.ascontiguousarray(words).reshape(g, 128, n, 2)
    nib = np.empty((g, 128, n, 4), np.uint8)
    nib[..., 0::2] = words & 0xF
    nib[..., 1::2] = words >> 4
    vals = E2M1[nib] * np.repeat(np.exp2(scales.astype(np.float64) - 127.0), 8, axis=1)[..., None]
    return vals.transpose(0, 1, 3, 2).reshape(g * 512, n)


K, T, S, D, N, H, V, U = 1024, 2048, 1024, 4, 128, 512, 256, 512


def setup_inputs():
    n = np.random.standard_normal
    s = mx_kscale(K)[:, None]
    u = mx_kscale(H)
    packed_xT = pack_weight(n((K, T)) * s)
    packed_w1 = pack_fp4(n((K, H)) / np.sqrt(K) / s)
    packed_w2 = pack_fp4(n((K, H)) / np.sqrt(K) / s)
    packed_w3 = pack_fp4(n((H, N)) / np.sqrt(H) / u[:, None])
    return {
        "x_words": packed_xT[0],
        "x_scales": packed_xT[1],
        "w1_words": packed_w1[0],
        "w1_scales": packed_w1[1],
        "w2_words": packed_w2[0],
        "w2_scales": packed_w2[1],
        "loss": (np.random.uniform(0.0, 2.0, (H, S))).astype(np.float32),
        "exp_": (np.random.uniform(0.3, 1.0, (H, S))).astype(np.float32),
        "unit": (np.random.uniform(0.6, 1.4, (H, 1)) * u[:, None]).astype(np.float32),
        "w3_words": packed_w3[0],
        "w3_scales": packed_w3[1],
        "offs": striped(np.random.permutation(T)[:S]),
        "seg": striped(np.random.permutation(np.concatenate([np.arange(V), np.random.randint(0, V, U - V)]))),
    }


def reference(x_words, x_scales, w1_words, w1_scales, w2_words, w2_scales, loss, exp_, unit, w3_words, w3_scales, offs, seg):
    xq = unpack_weight(x_words, x_scales)[:, unstriped(offs)]
    mu = unpack_fp4(w1_words, w1_scales).T @ xq
    mean_ = np.exp(1.6 * np.tanh(mu))
    rtmu = np.sqrt(mean_)
    devi = f64(loss) / rtmu + rtmu - (2.0 * f64(exp_))
    ph = unpack_fp4(w2_words, w2_scales).T @ xq
    disp = np.log(np.exp(ph) + 1.0) + 0.3
    wd = devi / disp
    grp = wd.reshape(len(wd), -1, D).mean(axis=2)
    mmean = mean_.reshape(len(mean_), -1, D).mean(axis=2)
    hid = f64(unit) * (grp[:, unstriped(seg)] * (np.sqrt(mmean[:, unstriped(seg)])))
    return unpack_fp4(w3_words, w3_scales).T @ mxq(hid, 0, "e4m3")

@@ -1,0 +1,323 @@
+from contextlib import ExitStack
+
+import concourse.mybir as mybir
+from concourse.masks import make_identity
+
+K, T, S, D, N, H, V, U = 1024, 2048, 1024, 4, 128, 512, 256, 512
+FLOPS = 2 * 2 * K * H * S + 2 * H * N * U
+
+F32 = mybir.dt.float32
+BF16 = mybir.dt.bfloat16
+I32 = mybir.dt.int32
+U32 = mybir.dt.uint32
+U16 = mybir.dt.uint16
+U8 = mybir.dt.uint8
+FP8X4 = mybir.dt.float8_e4m3fn_x4
+FP4X4 = mybir.dt.float4_e2m1fn_x4
+ALU = mybir.AluOpType
+ACT = mybir.ActivationFunctionType
+
+P = 128
+PASSES = 2
+HALF = 512
+HALVES = 2
+PACK = 4
+PIECE = 128
+JOINT = 2
+TINY = 2.0 ** -40
+
+
+def tile_picked_ytweed_root_p_kernel(
+    tc, x_words, x_scales, w1_words, w1_scales, w2_words, w2_scales, loss, exp_, unit,
+    w3_words, w3_scales, offs, seg, out,
+):
+    nc = tc.nc
+    with ExitStack() as ctx:
+        keep = ctx.enter_context(tc.tile_pool(name="keep", bufs=1))
+        psum = ctx.enter_context(tc.psum_pool(name="psum", bufs=8))
+
+        def held(shape, dtype, name, tag=None):
+            return keep.tile(shape, dtype, name=name, tag=tag or name, align_bytes=64)
+
+        def bank():
+            return psum.tile([P, 512], F32, name="bank")
+
+        def load_scales(queue, clear, src, name, tag=None):
+            passes, rows, cols = src.shape
+            plane = held([P, passes, cols], U8, name, tag)
+            clear.memset(plane[:].bitcast(I32), 0)
+            for q in range(4):
+                queue.dma_start(
+                    out=plane[32 * q : 32 * q + 4].bitcast(I32),
+                    in_=src[:, 4 * q : 4 * q + 4, :].rearrange("o r c -> r o c").bitcast(I32),
+                )
+            return plane
+
+        offs_sb = held([P, S // 16], U16, "offs_sb")
+        nc.sync.dma_start(offs_sb[:], offs)
+        ident_src = held([P, P], F32, "ident_src", "big_a1")
+        make_identity(nc, ident_src[:])
+        w1s_raw = load_scales(nc.gpsimd, nc.gpsimd, w1_scales, "w1s_raw", "big_a0")
+        xs = held([P, T], U8, "xs")
+        nc.vector.memset(xs[:].bitcast(I32), 0)
+        for q in range(4):
+            nc.sync.dma_start(
+                out=xs[32 * q : 32 * q + 8, :].bitcast(I32), in_=x_scales[:, 4 * q : 4 * q + 4, :].bitcast(I32)
+            )
+        gs = [held([P, S], U8, "gs%d" % o) for o in range(PASSES)]
+        nc.vector.memset(gs[1][:].bitcast(I32), 0)
+        ident = held([P, P], F32, "ident")
+        nc.vector.tensor_copy(out=ident[:], in_=ident_src[:])
+        w1_raw = held([P, PASSES, 2 * H], U8, "w1_raw")
+        nc.sync.dma_start(out=w1_raw[:].bitcast(I32), in_=w1_words.rearrange("o p c -> p o c").bitcast(I32))
+        xw = held([P, PASSES, T], U32, "xw", "big_a1")
+        for o in range(PASSES):
+            nc.sync.dma_start(out=xw[:, o, :].bitcast(I32), in_=x_words[o].rearrange("p n t -> p (n t)").bitcast(I32))
+        seg_sb = held([P, U // 16], U16, "seg_sb")
+        nc.sync.dma_start(seg_sb[:], seg)
+
+        gw = [[held([P, HALF], U32, "gw%d_%d" % (h, o)) for o in range(PASSES)] for h in range(HALVES)]
+        w1w = [held([P, PASSES, 2 * P], U8, "w1w%d" % t) for t in range(PACK)]
+        w1s = held([P, PACK, PASSES, P], U8, "w1s")
+
+        def gather_half(h):
+            piece = offs_sb[:, 32 * h : 32 * (h + 1)]
+            for o in range(PASSES):
+                nc.vector.tensor_copy(out=gw[h][o][:], in_=xw[:, o, :].indirect(piece))
+
+        def deal_w1(t):
+            nc.vector.tensor_copy(
+                out=w1w[t][:].rearrange("p o (m b) -> p o m b", b=2),
+                in_=w1_raw[:].rearrange("p o (m t b) -> p o m t b", t=PACK, b=2)[:, :, :, t, :],
+            )
+
+        th = [held([P, PACK, HALF], F32, "th%d" % h) for h in range(HALVES)]
+        mean = [held([P, PACK, HALF], F32, "mean%d" % h) for h in range(HALVES)]
+        irt = [held([P, PACK, HALF], F32, "irt%d" % h) for h in range(HALVES)]
+        num = [held([P, PACK, HALF], F32, "num%d" % h) for h in range(HALVES)]
+        m2e = [held([P, PACK, HALF], F32, "m2e%d" % h) for h in range(HALVES)]
+        msum = held([P, PACK, V], F32, "msum")
+
+        def mean_side(h):
+            for t in range(PACK):
+                mu = bank()
+                for o in range(PASSES):
+                    nc.tensor.matmul_mx(
+                        out=mu[:],
+                        lhsT=w1w[t][:, o, :].bitcast(FP4X4), lhsT_scale=w1s[:, t, o, :],
+                        rhs=gw[h][o][:].bitcast(FP8X4), rhs_scale=gs[o][:, HALF * h : HALF * (h + 1)],
+                        start=(o == 0), stop=(o == PASSES - 1),
+                    )
+                nc.scalar.activation(
+                    out=th[h][:, t, :].rearrange("p (d v) -> p d v", d=D),
+                    in_=mu[:].rearrange("p (v d) -> p d v", d=D), func=ACT.Tanh,
+                )
+                nc.scalar.activation(out=mean[h][:, t, :], in_=th[h][:, t, :], func=ACT.Exp, scale=1.6)
+                nc.scalar.activation(out=irt[h][:, t, :], in_=th[h][:, t, :], func=ACT.Exp, scale=-0.8)
+
+        def by_member(ap):
+            return ap.rearrange("p (d c i) -> p c d i", d=D, i=4)
+
+        def by_entry(ap):
+            return ap.rearrange("p (c i d) -> p c d i", d=D, i=4)
+
+        for t in range(PACK):
+            deal_w1(t)
+        nc.vector.tensor_copy(out=gs[0][:], in_=xs[:].indirect(offs_sb[:]))
+        for q in range(4):
+            nc.scalar.dma_start(
+                out=gs[1][32 * q : 32 * q + 4, :].bitcast(I32), in_=gs[0][32 * q + 4 : 32 * q + 8, :].bitcast(I32)
+            )
+        gather_half(0)
+        nc.vector.tensor_copy(
+            out=w1s[:].rearrange("p t o m -> p o t m"), in_=w1s_raw[:].rearrange("p o (m t) -> p o t m", t=PACK)
+        )
+        gather_half(1)
+
+        loss_raw, exp_raw = [], []
+        for h in range(HALVES):
+            t_ = held([P, PACK, HALF], F32, "loss_raw%d" % h, "big_a%d" % h)
+            nc.sync.dma_start(out=t_[:], in_=loss.rearrange("(p t) j -> p t j", t=PACK)[:, :, HALF * h : HALF * (h + 1)])
+            loss_raw.append(t_)
+        w2w = held([P, PASSES, 2 * H], U8, "w2w", "w1_raw")
+        nc.sync.dma_start(out=w2w[:].bitcast(I32), in_=w2_words.rearrange("o p c -> p o c").bitcast(I32))
+        w2s = load_scales(nc.sync, nc.gpsimd, w2_scales, "w2s", "xs")
+        mean_side(0)
+        mean_side(1)
+
+        dw = [[held([P, HALF], U32, "dw%d_%d" % (h, o), "w1w%d" % (2 * h + o)) for o in range(PASSES)] for h in range(HALVES)]
+        dsc = held([P, HALVES, PASSES, HALF], U8, "dsc", "w1s")
+        for h in range(HALVES):
+            for o in range(PASSES):
+                nc.vector.tensor_copy(out=by_member(dw[h][o][:].bitcast(I32)), in_=by_entry(gw[h][o][:].bitcast(I32)))
+                nc.vector.tensor_copy(out=by_member(dsc[:, h, o, :]), in_=by_entry(gs[o][:, HALF * h : HALF * (h + 1)]))
+
+        for h in range(HALVES):
+            t_ = held([P, PACK, HALF], F32, "exp_raw%d" % h, "gw0_%d" % h)
+            nc.sync.dma_start(out=t_[:], in_=exp_.rearrange("(p t) j -> p t j", t=PACK)[:, :, HALF * h : HALF * (h + 1)])
+            exp_raw.append(t_)
+        unit_sb = held([P, PACK], F32, "unit_sb", "gs0")
+        nc.sync.dma_start(out=unit_sb[:], in_=unit.rearrange("(p t) o -> p (t o)", t=PACK))
+        w3w = held([P, 2 * N], U8, "w3w", "gw1_0")
+        nc.sync.dma_start(out=w3w[:].bitcast(I32), in_=w3_words[0].bitcast(I32))
+        w3s = load_scales(nc.sync, nc.gpsimd, w3_scales, "w3s", "gw1_1")
+
+        pair = [held([P, PACK, 2 * P], F32, "pair%d" % h) for h in range(HALVES)]
+        for h in range(HALVES):
+            for t in range(PACK):
+                nc.vector.tensor_copy(out=by_member(num[h][:, t, :]), in_=by_entry(loss_raw[h][:, t, :]))
+            nc.vector.tensor_tensor(out=pair[h][:], in0=mean[h][:, :, : 2 * P], in1=mean[h][:, :, 2 * P :], op=ALU.add)
+            nc.vector.tensor_tensor(out=num[h][:], in0=num[h][:], in1=mean[h][:], op=ALU.add)
+            nc.vector.tensor_tensor(
+                out=msum[:, :, P * h : P * (h + 1)], in0=pair[h][:, :, :P], in1=pair[h][:, :, P:], op=ALU.add
+            )
+
+        for h in range(HALVES):
+            nc.vector.tensor_tensor(out=num[h][:], in0=num[h][:], in1=irt[h][:], op=ALU.mult)
+            for t in range(PACK):
+                nc.vector.tensor_scalar(
+                    out=by_member(m2e[h][:, t, :]), in0=by_entry(exp_raw[h][:, t, :]),
+                    scalar1=-2.0, scalar2=None, op0=ALU.mult,
+                )
+
+        ph = []
+        sig = [held([P, D, H], F32, "sig%d" % h, "big_a%d" % h) for h in range(HALVES)]
+        lg = held([P, HALVES * D, H], F32, "lg")
+        for h in range(HALVES):
+            for d in range(D):
+                acc = bank()
+                for o in range(PASSES):
+                    nc.tensor.matmul_mx(
+                        out=acc[:],
+                        lhsT=dw[h][o][:, P * d : P * (d + 1)].bitcast(FP8X4), lhsT_scale=dsc[:, h, o, P * d : P * (d + 1)],
+                        rhs=w2w[:, o, :].bitcast(FP4X4), rhs_scale=w2s[:, o, :],
+                        start=(o == 0), stop=(o == PASSES - 1),
+                    )
+                ph.append(acc)
+                nc.scalar.activation(
+                    out=sig[h][:, d, :].rearrange("p (t m) -> p t m", t=PACK),
+                    in_=acc[:].rearrange("p (m t) -> p t m", t=PACK), func=ACT.Sigmoid, scale=-1.0,
+                )
+        for h in range(HALVES):
+            for d in range(D):
+                b = D * h + d
+                nc.scalar.activation(out=lg[:, b, :], in_=sig[h][:, d, :], func=ACT.Ln, bias=TINY)
+                nc.vector.scalar_tensor_tensor(
+                    out=sig[h][:, d, :].rearrange("p (t m) -> p t m", t=PACK),
+                    in0=lg[:, b, :].rearrange("p (t m) -> p t m", t=PACK), scalar=-1.0,
+                    in1=ph[b][:].rearrange("p (m t) -> p t m", t=PACK), op0=ALU.mult, op1=ALU.max,
+                )
+        split = JOINT * P
+        for h in range(HALVES):
+            nc.scalar.activation(out=lg[:, D * h : D * (h + 1), split:], in_=sig[h][:, :, split:], func=ACT.Ln, bias=0.3)
+        lm = held([P, PACK, V], F32, "lm")
+        nc.scalar.activation(out=lm[:], in_=msum[:], func=ACT.Ln, scale=1.0 / 64.0)
+
+        odd = held([P, HALVES, 2, split], F32, "odd", "th0")
+        prod2 = held([P, HALVES, 2, split], F32, "prod2", "th1")
+        prod4 = held([P, HALVES, split], F32, "prod4", "pair0")
+        cof = held([P, HALVES, D, split], F32, "cof", "mean0")
+        for h in range(HALVES):
+            nc.vector.tensor_scalar(out=odd[:, h], in0=sig[h][:, 1::2, :split], scalar1=0.3, scalar2=None, op0=ALU.add)
+        for h in range(HALVES):
+            nc.vector.scalar_tensor_tensor(
+                out=prod2[:, h], in0=sig[h][:, 0::2, :split], scalar=0.3, in1=odd[:, h], op0=ALU.add, op1=ALU.mult
+            )
+        nc.vector.tensor_tensor(out=prod4[:], in0=prod2[:, :, 0, :], in1=prod2[:, :, 1, :], op=ALU.mult)
+        lp = held([P, HALVES, split], F32, "lp", "pair1")
+        nc.scalar.activation(out=lp[:], in_=prod4[:], func=ACT.Ln)
+        for h in range(HALVES):
+            for a in range(2):
+                nc.vector.tensor_tensor(out=cof[:, h, 2 * a, :], in0=odd[:, h, a, :], in1=prod2[:, h, 1 - a, :], op=ALU.mult)
+                nc.vector.scalar_tensor_tensor(
+                    out=cof[:, h, 2 * a + 1, :], in0=sig[h][:, 2 * a, :split], scalar=0.3, in1=prod2[:, h, 1 - a, :],
+                    op0=ALU.add, op1=ALU.mult,
+                )
+
+        def deviance(t, h):
+            acc = bank()
+            for d in range(D):
+                cols = slice(P * d, P * (d + 1))
+                nc.tensor.matmul(out=acc[:, cols], lhsT=m2e[h][:, t, cols], rhs=ident[:], is_transpose=True, start=True, stop=False)
+                nc.tensor.matmul(out=acc[:, cols], lhsT=num[h][:, t, cols], rhs=ident[:], is_transpose=True, start=False, stop=True)
+            return acc
+
+        devi = {}
+        for t in range(JOINT):
+            for h in range(HALVES):
+                devi[t, h] = deviance(t, h)
+        lpt = bank()
+        for t in range(JOINT):
+            for h in range(HALVES):
+                nc.tensor.transpose(lpt[:, V * t + P * h : V * t + P * (h + 1)], lp[:, h, P * t : P * (t + 1)], ident[:])
+        expo = held([P, JOINT * V], F32, "expo")
+        nc.vector.scalar_tensor_tensor(
+            out=expo[:], in0=lm[:, :JOINT, :].rearrange("p t v -> p (t v)"), scalar=0.5, in1=lpt[:, : JOINT * V],
+            op0=ALU.mult, op1=ALU.subtract,
+        )
+        devi[2, 0] = deviance(2, 0)
+        devi[2, 1] = deviance(2, 1)
+        devi[3, 0] = deviance(3, 0)
+
+        late = held([P, PACK - JOINT + 1, HALVES * HALF], F32, "late", "pair0")
+        fac = late[:, 0, :].rearrange("p (t v) -> p t v", t=PACK)
+        rinv = {}
+        for t in range(JOINT, PACK):
+            rinv[t] = late[:, 1 + t - JOINT, :].rearrange("p (h d m) -> p h d m", h=HALVES, d=D)
+            nc.scalar.activation(
+                out=rinv[t].rearrange("p h d m -> p (h d) m"), in_=lg[:, :, P * t : P * (t + 1)], func=ACT.Exp, scale=-1.0
+            )
+            if t == JOINT:
+                nc.scalar.activation(out=fac[:, :JOINT, :].rearrange("p t v -> p (t v)"), in_=expo[:], func=ACT.Exp)
+        nc.scalar.activation(out=fac[:, JOINT:, :], in_=lm[:, JOINT:, :], func=ACT.Exp, scale=0.5)
+
+        planes = held([P, PACK, U], BF16, "planes")
+        vals = []
+        for t in range(PACK):
+            wd = held([P, HALVES, D, P], F32, "wd%d" % t, "irt%d" % (t % 2))
+            grp = bank()
+            if t == 1:
+                devi[3, 1] = deviance(3, 1)
+            for h in range(HALVES):
+                weight = cof[:, h, :, P * t : P * (t + 1)] if t < JOINT else rinv[t][:, h]
+                nc.vector.tensor_tensor(
+                    out=wd[:, h], in0=devi[t, h][:].rearrange("p (d m) -> p d m", d=D), in1=weight, op=ALU.mult
+                )
+                for d in range(D):
+                    nc.tensor.matmul(
+                        out=grp[:, P * h : P * (h + 1)], lhsT=wd[:, h, d, :], rhs=ident[:],
+                        is_transpose=True, start=(d == 0), stop=(d == D - 1),
+                    )
+            val = held([P, V], F32, "val%d" % t)
+            nc.vector.scalar_tensor_tensor(
+                out=val[:], in0=grp[:, :V], scalar=unit_sb[:, t : t + 1], in1=fac[:, t, :], op0=ALU.mult, op1=ALU.mult
+            )
+            vals.append(val)
+
+        for t in range(PACK):
+            for q in range(U // PIECE):
+                looked_up = vals[t][:].indirect(seg_sb[:, 8 * q : 8 * (q + 1)])
+                dst = planes[:, t, PIECE * q : PIECE * (q + 1)]
+                if t < PACK - 1:
+                    nc.scalar.activation(out=dst, in_=looked_up, func=ACT.Copy)
+                else:
+                    nc.vector.tensor_copy(out=dst, in_=looked_up)
+
+        for c in range(2):
+            cols = slice(256 * c, 256 * (c + 1))
+            hid = held([P, 256, PACK], BF16, "hid%d" % c)
+            nc.vector.tensor_copy(
+                out=hid[:].rearrange("p (c i) t -> p c t i", i=4),
+                in_=planes[:, :, cols].rearrange("p t (c i) -> p c t i", i=4),
+            )
+            codes = held([P, 256], U32, "codes%d" % c)
+            scales = held([P, 256], U8, "scales%d" % c)
+            nc.vector.quantize_mx(out=codes[:].bitcast(FP8X4), scales=scales[:], in_=hid[:].rearrange("p r t -> p (r t)"))
+            acc = bank()
+            nc.tensor.matmul_mx(
+                out=acc[:, :256], lhsT=w3w[:].bitcast(FP4X4), lhsT_scale=w3s[:, 0, :],
+                rhs=codes[:].bitcast(FP8X4), rhs_scale=scales[:], start=True, stop=True,
+            )
+            res = held([P, 256], F32, "res%d" % c)
+            nc.scalar.copy(out=res[:], in_=acc[:, :256])
+            nc.sync.dma_start(out=out[:, cols], in_=res[:])

@@ -42,37 +42,35 @@ def tile_picked_ytweed_root_p_kernel(
         def bank():
             return psum.tile([P, 512], F32, name="bank")
 
-        def load_scales(queue, clear, src, name, tag=None):
-            passes, rows, cols = src.shape
-            plane = held([P, passes, cols], U8, name, tag)
-            clear.memset(plane[:].bitcast(I32), 0)
+        def load_rows(plane, src):
             for q in range(4):
-                queue.dma_start(
-                    out=plane[32 * q : 32 * q + 4].bitcast(I32),
+                nc.sync.dma_start(
+                    out=plane[32 * q : 32 * q + 4, :].bitcast(I32),
                     in_=src[:, 4 * q : 4 * q + 4, :].rearrange("o r c -> r o c").bitcast(I32),
                 )
+
+        def load_scales(clear, src, name, tag=None):
+            passes, rows, cols = src.shape
+            plane = held([P, passes * cols], U8, name, tag)
+            clear.memset(plane[:].bitcast(I32), 0)
+            load_rows(plane, src)
             return plane
 
         offs_sb = held([P, S // 16], U16, "offs_sb")
         nc.sync.dma_start(offs_sb[:], offs)
-        ident_src = held([P, P], F32, "ident_src", "big_a1")
-        make_identity(nc, ident_src[:])
-        w1s_raw = load_scales(nc.gpsimd, nc.gpsimd, w1_scales, "w1s_raw", "big_a0")
-        xs = held([P, T], U8, "xs")
-        nc.vector.memset(xs[:].bitcast(I32), 0)
-        for q in range(4):
-            nc.sync.dma_start(
-                out=xs[32 * q : 32 * q + 8, :].bitcast(I32), in_=x_scales[:, 4 * q : 4 * q + 4, :].bitcast(I32)
-            )
-        gs = [held([P, S], U8, "gs%d" % o) for o in range(PASSES)]
-        nc.vector.memset(gs[1][:].bitcast(I32), 0)
+        xs = load_scales(nc.vector, x_scales, "xs")
+        zeros = held([P, PASSES * H // 4], I32, "zeros", "big_a1")
+        nc.vector.memset(zeros[:], 0)
+        w1s_raw = held([P, PASSES * H], U8, "w1s_raw")
+        nc.vector.tensor_copy(out=w1s_raw[:].bitcast(I32), in_=zeros[:])
         ident = held([P, P], F32, "ident")
-        nc.vector.tensor_copy(out=ident[:], in_=ident_src[:])
+        make_identity(nc, ident[:])
         w1_raw = held([P, PASSES, 2 * H], U8, "w1_raw")
         nc.sync.dma_start(out=w1_raw[:].bitcast(I32), in_=w1_words.rearrange("o p c -> p o c").bitcast(I32))
-        xw = held([P, PASSES, T], U32, "xw", "big_a1")
-        for o in range(PASSES):
-            nc.sync.dma_start(out=xw[:, o, :].bitcast(I32), in_=x_words[o].rearrange("p n t -> p (n t)").bitcast(I32))
+        xw = held([P, PASSES * T], U32, "xw", "big_a1")
+        nc.sync.dma_start(out=xw[:, :T].bitcast(I32), in_=x_words[0].rearrange("p n t -> p (n t)").bitcast(I32))
+        load_rows(w1s_raw, w1_scales)
+        nc.sync.dma_start(out=xw[:, T:].bitcast(I32), in_=x_words[1].rearrange("p n t -> p (n t)").bitcast(I32))
         seg_sb = held([P, U // 16], U16, "seg_sb")
         nc.sync.dma_start(seg_sb[:], seg)
 
@@ -83,7 +81,9 @@ def tile_picked_ytweed_root_p_kernel(
         def gather_half(h):
             piece = offs_sb[:, 32 * h : 32 * (h + 1)]
             for o in range(PASSES):
-                nc.vector.tensor_copy(out=gw[h][o][:], in_=xw[:, o, :].indirect(piece))
+                nc.vector.tensor_copy(out=gs[h][:, o, :], in_=xs[:, T * o : T * (o + 1)].indirect(piece))
+            for o in range(PASSES):
+                nc.vector.tensor_copy(out=gw[h][o][:], in_=xw[:, T * o : T * (o + 1)].indirect(piece))
 
         def deal_w1(t):
             nc.vector.tensor_copy(
@@ -95,7 +95,6 @@ def tile_picked_ytweed_root_p_kernel(
         mean = [held([P, PACK, HALF], F32, "mean%d" % h) for h in range(HALVES)]
         irt = [held([P, PACK, HALF], F32, "irt%d" % h) for h in range(HALVES)]
         num = [held([P, PACK, HALF], F32, "num%d" % h) for h in range(HALVES)]
-        m2e = [held([P, PACK, HALF], F32, "m2e%d" % h) for h in range(HALVES)]
         msum = held([P, PACK, V], F32, "msum")
 
         def mean_side(h):
@@ -105,7 +104,7 @@ def tile_picked_ytweed_root_p_kernel(
                     nc.tensor.matmul_mx(
                         out=mu[:],
                         lhsT=w1w[t][:, o, :].bitcast(FP4X4), lhsT_scale=w1s[:, t, o, :],
-                        rhs=gw[h][o][:].bitcast(FP8X4), rhs_scale=gs[o][:, HALF * h : HALF * (h + 1)],
+                        rhs=gw[h][o][:].bitcast(FP8X4), rhs_scale=gs[h][:, o, :],
                         start=(o == 0), stop=(o == PASSES - 1),
                     )
                 nc.scalar.activation(
@@ -123,25 +122,23 @@ def tile_picked_ytweed_root_p_kernel(
 
         for t in range(PACK):
             deal_w1(t)
-        nc.vector.tensor_copy(out=gs[0][:], in_=xs[:].indirect(offs_sb[:]))
-        for q in range(4):
-            nc.scalar.dma_start(
-                out=gs[1][32 * q : 32 * q + 4, :].bitcast(I32), in_=gs[0][32 * q + 4 : 32 * q + 8, :].bitcast(I32)
-            )
+        gs = [held([P, PASSES, HALF], U8, "gs0")]
         gather_half(0)
-        nc.vector.tensor_copy(
-            out=w1s[:].rearrange("p t o m -> p o t m"), in_=w1s_raw[:].rearrange("p o (m t) -> p o t m", t=PACK)
-        )
+        for ts in (slice(0, 1), slice(1, PACK)):
+            nc.vector.tensor_copy(
+                out=w1s[:, ts].rearrange("p t o m -> p o t m"),
+                in_=w1s_raw[:].rearrange("p (o m t) -> p o t m", o=PASSES, t=PACK)[:, :, ts, :],
+            )
+        gs.append(held([P, PASSES, HALF], U8, "gs1", "big_a1"))
         gather_half(1)
 
         loss_raw, exp_raw = [], []
         for h in range(HALVES):
-            t_ = held([P, PACK, HALF], F32, "loss_raw%d" % h, "big_a%d" % h)
+            t_ = held([P, PACK, HALF], F32, "loss_raw%d" % h, ("w1_raw", "w1s_raw")[h])
             nc.sync.dma_start(out=t_[:], in_=loss.rearrange("(p t) j -> p t j", t=PACK)[:, :, HALF * h : HALF * (h + 1)])
             loss_raw.append(t_)
-        w2w = held([P, PASSES, 2 * H], U8, "w2w", "w1_raw")
+        w2w = held([P, PASSES, 2 * H], U8, "w2w", "xs")
         nc.sync.dma_start(out=w2w[:].bitcast(I32), in_=w2_words.rearrange("o p c -> p o c").bitcast(I32))
-        w2s = load_scales(nc.sync, nc.gpsimd, w2_scales, "w2s", "xs")
         mean_side(0)
         mean_side(1)
 
@@ -150,38 +147,37 @@ def tile_picked_ytweed_root_p_kernel(
         for h in range(HALVES):
             for o in range(PASSES):
                 nc.vector.tensor_copy(out=by_member(dw[h][o][:].bitcast(I32)), in_=by_entry(gw[h][o][:].bitcast(I32)))
-                nc.vector.tensor_copy(out=by_member(dsc[:, h, o, :]), in_=by_entry(gs[o][:, HALF * h : HALF * (h + 1)]))
+                nc.vector.tensor_copy(out=by_member(dsc[:, h, o, :]), in_=by_entry(gs[h][:, o, :]))
 
+        w2s = load_scales(nc.gpsimd, w2_scales, "w2s", "gw0_0")
         for h in range(HALVES):
-            t_ = held([P, PACK, HALF], F32, "exp_raw%d" % h, "gw0_%d" % h)
+            t_ = held([P, PACK, HALF], F32, "exp_raw%d" % h, "gw%d_1" % h)
             nc.sync.dma_start(out=t_[:], in_=exp_.rearrange("(p t) j -> p t j", t=PACK)[:, :, HALF * h : HALF * (h + 1)])
             exp_raw.append(t_)
         unit_sb = held([P, PACK], F32, "unit_sb", "gs0")
         nc.sync.dma_start(out=unit_sb[:], in_=unit.rearrange("(p t) o -> p (t o)", t=PACK))
+        neg_unit = held([P, PACK], F32, "neg_unit")
+        nc.gpsimd.tensor_scalar(out=neg_unit[:], in0=unit_sb[:], scalar1=-1.0, scalar2=0.0, op0=ALU.mult, op1=ALU.add)
         w3w = held([P, 2 * N], U8, "w3w", "gw1_0")
         nc.sync.dma_start(out=w3w[:].bitcast(I32), in_=w3_words[0].bitcast(I32))
-        w3s = load_scales(nc.sync, nc.gpsimd, w3_scales, "w3s", "gw1_1")
+        w3s = load_scales(nc.gpsimd, w3_scales, "w3s", "big_a1")
 
         pair = [held([P, PACK, 2 * P], F32, "pair%d" % h) for h in range(HALVES)]
         for h in range(HALVES):
-            for t in range(PACK):
-                nc.vector.tensor_copy(out=by_member(num[h][:, t, :]), in_=by_entry(loss_raw[h][:, t, :]))
             nc.vector.tensor_tensor(out=pair[h][:], in0=mean[h][:, :, : 2 * P], in1=mean[h][:, :, 2 * P :], op=ALU.add)
-            nc.vector.tensor_tensor(out=num[h][:], in0=num[h][:], in1=mean[h][:], op=ALU.add)
+            for t in range(PACK):
+                nc.vector.tensor_tensor(
+                    out=by_member(num[h][:, t, :]), in0=by_entry(loss_raw[h][:, t, :]), in1=by_member(mean[h][:, t, :]), op=ALU.add
+                )
             nc.vector.tensor_tensor(
                 out=msum[:, :, P * h : P * (h + 1)], in0=pair[h][:, :, :P], in1=pair[h][:, :, P:], op=ALU.add
             )
-
-        for h in range(HALVES):
-            nc.vector.tensor_tensor(out=num[h][:], in0=num[h][:], in1=irt[h][:], op=ALU.mult)
-            for t in range(PACK):
-                nc.vector.tensor_scalar(
-                    out=by_member(m2e[h][:, t, :]), in0=by_entry(exp_raw[h][:, t, :]),
-                    scalar1=-2.0, scalar2=None, op0=ALU.mult,
-                )
+            nc.vector.scalar_tensor_tensor(
+                out=num[h][:], in0=num[h][:], scalar=-0.5, in1=irt[h][:], op0=ALU.mult, op1=ALU.mult
+            )
 
         ph = []
-        sig = [held([P, D, H], F32, "sig%d" % h, "big_a%d" % h) for h in range(HALVES)]
+        sig = [held([P, D, H], F32, "sig%d" % h, ("w1_raw", "w1s_raw")[h]) for h in range(HALVES)]
         lg = held([P, HALVES * D, H], F32, "lg")
         for h in range(HALVES):
             for d in range(D):
@@ -190,7 +186,7 @@ def tile_picked_ytweed_root_p_kernel(
                     nc.tensor.matmul_mx(
                         out=acc[:],
                         lhsT=dw[h][o][:, P * d : P * (d + 1)].bitcast(FP8X4), lhsT_scale=dsc[:, h, o, P * d : P * (d + 1)],
-                        rhs=w2w[:, o, :].bitcast(FP4X4), rhs_scale=w2s[:, o, :],
+                        rhs=w2w[:, o, :].bitcast(FP4X4), rhs_scale=w2s[:, H * o : H * (o + 1)],
                         start=(o == 0), stop=(o == PASSES - 1),
                     )
                 ph.append(acc)
@@ -211,7 +207,7 @@ def tile_picked_ytweed_root_p_kernel(
         for h in range(HALVES):
             nc.scalar.activation(out=lg[:, D * h : D * (h + 1), split:], in_=sig[h][:, :, split:], func=ACT.Ln, bias=0.3)
         lm = held([P, PACK, V], F32, "lm")
-        nc.scalar.activation(out=lm[:], in_=msum[:], func=ACT.Ln, scale=1.0 / 64.0)
+        nc.scalar.activation(out=lm[:], in_=msum[:], func=ACT.Ln, scale=1.0 / 16.0)
 
         odd = held([P, HALVES, 2, split], F32, "odd", "th0")
         prod2 = held([P, HALVES, 2, split], F32, "prod2", "th1")
@@ -238,26 +234,11 @@ def tile_picked_ytweed_root_p_kernel(
             acc = bank()
             for d in range(D):
                 cols = slice(P * d, P * (d + 1))
-                nc.tensor.matmul(out=acc[:, cols], lhsT=m2e[h][:, t, cols], rhs=ident[:], is_transpose=True, start=True, stop=False)
+                nc.tensor.matmul(out=acc[:, cols], lhsT=exp_raw[h][:, t, d::D], rhs=ident[:], is_transpose=True, start=True, stop=False)
                 nc.tensor.matmul(out=acc[:, cols], lhsT=num[h][:, t, cols], rhs=ident[:], is_transpose=True, start=False, stop=True)
             return acc
 
-        devi = {}
-        for t in range(JOINT):
-            for h in range(HALVES):
-                devi[t, h] = deviance(t, h)
-        lpt = bank()
-        for t in range(JOINT):
-            for h in range(HALVES):
-                nc.tensor.transpose(lpt[:, V * t + P * h : V * t + P * (h + 1)], lp[:, h, P * t : P * (t + 1)], ident[:])
-        expo = held([P, JOINT * V], F32, "expo")
-        nc.vector.scalar_tensor_tensor(
-            out=expo[:], in0=lm[:, :JOINT, :].rearrange("p t v -> p (t v)"), scalar=0.5, in1=lpt[:, : JOINT * V],
-            op0=ALU.mult, op1=ALU.subtract,
-        )
-        devi[2, 0] = deviance(2, 0)
-        devi[2, 1] = deviance(2, 1)
-        devi[3, 0] = deviance(3, 0)
+        devi = {(t, h): deviance(t, h) for t in range(PACK) for h in range(HALVES)}
 
         late = held([P, PACK - JOINT + 1, HALVES * HALF], F32, "late", "pair0")
         fac = late[:, 0, :].rearrange("p (t v) -> p t v", t=PACK)
@@ -267,30 +248,47 @@ def tile_picked_ytweed_root_p_kernel(
             nc.scalar.activation(
                 out=rinv[t].rearrange("p h d m -> p (h d) m"), in_=lg[:, :, P * t : P * (t + 1)], func=ACT.Exp, scale=-1.0
             )
-            if t == JOINT:
-                nc.scalar.activation(out=fac[:, :JOINT, :].rearrange("p t v -> p (t v)"), in_=expo[:], func=ACT.Exp)
         nc.scalar.activation(out=fac[:, JOINT:, :], in_=lm[:, JOINT:, :], func=ACT.Exp, scale=0.5)
 
         planes = held([P, PACK, U], BF16, "planes")
-        vals = []
-        for t in range(PACK):
-            wd = held([P, HALVES, D, P], F32, "wd%d" % t, "irt%d" % (t % 2))
+        wd = [held([P, HALVES, D, P], F32, "wd%d" % t, ("irt0", "irt1", "mean1", "wd3")[t]) for t in range(PACK)]
+
+        def weigh(t, h):
+            weight = cof[:, h, :, P * t : P * (t + 1)] if t < JOINT else rinv[t][:, h]
+            nc.vector.tensor_tensor(
+                out=wd[t][:, h], in0=devi[t, h][:].rearrange("p (d m) -> p d m", d=D), in1=weight, op=ALU.mult
+            )
+
+        def group_sums(t):
             grp = bank()
-            if t == 1:
-                devi[3, 1] = deviance(3, 1)
             for h in range(HALVES):
-                weight = cof[:, h, :, P * t : P * (t + 1)] if t < JOINT else rinv[t][:, h]
-                nc.vector.tensor_tensor(
-                    out=wd[:, h], in0=devi[t, h][:].rearrange("p (d m) -> p d m", d=D), in1=weight, op=ALU.mult
-                )
                 for d in range(D):
                     nc.tensor.matmul(
-                        out=grp[:, P * h : P * (h + 1)], lhsT=wd[:, h, d, :], rhs=ident[:],
+                        out=grp[:, P * h : P * (h + 1)], lhsT=wd[t][:, h, d, :], rhs=ident[:],
                         is_transpose=True, start=(d == 0), stop=(d == D - 1),
                     )
+            return grp
+
+        weigh(0, 0)
+        lpt = bank()
+        for t in range(JOINT):
+            for h in range(HALVES):
+                nc.tensor.transpose(lpt[:, V * t + P * h : V * t + P * (h + 1)], lp[:, h, P * t : P * (t + 1)], ident[:])
+        weigh(0, 1)
+        joint = lm[:, :JOINT, :].rearrange("p t v -> p (t v)")
+        nc.vector.scalar_tensor_tensor(
+            out=joint, in0=lpt[:, : JOINT * V], scalar=-2.0, in1=joint, op0=ALU.mult, op1=ALU.add
+        )
+        nc.scalar.activation(out=fac[:, :JOINT, :], in_=lm[:, :JOINT, :], func=ACT.Exp, scale=0.5)
+        vals = []
+        for t in range(PACK):
+            grp = group_sums(t)
+            if t + 1 < PACK:
+                weigh(t + 1, 0)
+                weigh(t + 1, 1)
             val = held([P, V], F32, "val%d" % t)
             nc.vector.scalar_tensor_tensor(
-                out=val[:], in0=grp[:, :V], scalar=unit_sb[:, t : t + 1], in1=fac[:, t, :], op0=ALU.mult, op1=ALU.mult
+                out=val[:], in0=grp[:, :V], scalar=neg_unit[:, t : t + 1], in1=fac[:, t, :], op0=ALU.mult, op1=ALU.mult
             )
             vals.append(val)
 
@@ -315,7 +313,7 @@ def tile_picked_ytweed_root_p_kernel(
             nc.vector.quantize_mx(out=codes[:].bitcast(FP8X4), scales=scales[:], in_=hid[:].rearrange("p r t -> p (r t)"))
             acc = bank()
             nc.tensor.matmul_mx(
-                out=acc[:, :256], lhsT=w3w[:].bitcast(FP4X4), lhsT_scale=w3s[:, 0, :],
+                out=acc[:, :256], lhsT=w3w[:].bitcast(FP4X4), lhsT_scale=w3s[:],
                 rhs=codes[:].bitcast(FP8X4), rhs_scale=scales[:], start=True, stop=True,
             )
             res = held([P, 256], F32, "res%d" % c)

from contextlib import ExitStack

import concourse.mybir as mybir
from concourse.masks import make_identity

K, T, S, D, N, H, V, U = 1024, 2048, 1024, 4, 128, 512, 256, 512
FLOPS = 2 * 2 * K * H * S + 2 * H * N * U

F32 = mybir.dt.float32
BF16 = mybir.dt.bfloat16
I32 = mybir.dt.int32
U32 = mybir.dt.uint32
U16 = mybir.dt.uint16
U8 = mybir.dt.uint8
FP8X4 = mybir.dt.float8_e4m3fn_x4
FP4X4 = mybir.dt.float4_e2m1fn_x4
ALU = mybir.AluOpType
ACT = mybir.ActivationFunctionType

P = 128
PASSES = 2
HALF = 512
HALVES = 2
PACK = 4
PIECE = 128
JOINT = 2
TINY = 2.0 ** -40


def tile_picked_ytweed_root_p_kernel(
    tc, x_words, x_scales, w1_words, w1_scales, w2_words, w2_scales, loss, exp_, unit,
    w3_words, w3_scales, offs, seg, out,
):
    nc = tc.nc
    with ExitStack() as ctx:
        keep = ctx.enter_context(tc.tile_pool(name="keep", bufs=1))
        psum = ctx.enter_context(tc.psum_pool(name="psum", bufs=8))

        def held(shape, dtype, name, tag=None):
            return keep.tile(shape, dtype, name=name, tag=tag or name, align_bytes=64)

        def bank():
            return psum.tile([P, 512], F32, name="bank")

        def load_rows(plane, src):
            for q in range(4):
                nc.sync.dma_start(
                    out=plane[32 * q : 32 * q + 4, :].bitcast(I32),
                    in_=src[:, 4 * q : 4 * q + 4, :].rearrange("o r c -> r o c").bitcast(I32),
                )

        def load_scales(clear, src, name, tag=None):
            passes, rows, cols = src.shape
            plane = held([P, passes * cols], U8, name, tag)
            clear.memset(plane[:].bitcast(I32), 0)
            load_rows(plane, src)
            return plane

        offs_sb = held([P, S // 16], U16, "offs_sb")
        nc.sync.dma_start(offs_sb[:], offs)
        xs = load_scales(nc.vector, x_scales, "xs")
        zeros = held([P, PASSES * H // 4], I32, "zeros", "big_a1")
        nc.vector.memset(zeros[:], 0)
        w1s_raw = held([P, PASSES * H], U8, "w1s_raw")
        nc.vector.tensor_copy(out=w1s_raw[:].bitcast(I32), in_=zeros[:])
        ident = held([P, P], F32, "ident")
        make_identity(nc, ident[:])
        w1_raw = held([P, PASSES, 2 * H], U8, "w1_raw")
        nc.sync.dma_start(out=w1_raw[:].bitcast(I32), in_=w1_words.rearrange("o p c -> p o c").bitcast(I32))
        xw = held([P, PASSES * T], U32, "xw", "big_a1")
        nc.sync.dma_start(out=xw[:, :T].bitcast(I32), in_=x_words[0].rearrange("p n t -> p (n t)").bitcast(I32))
        load_rows(w1s_raw, w1_scales)
        nc.sync.dma_start(out=xw[:, T:].bitcast(I32), in_=x_words[1].rearrange("p n t -> p (n t)").bitcast(I32))
        seg_sb = held([P, U // 16], U16, "seg_sb")
        nc.sync.dma_start(seg_sb[:], seg)

        gw = [[held([P, HALF], U32, "gw%d_%d" % (h, o)) for o in range(PASSES)] for h in range(HALVES)]
        w1w = [held([P, PASSES, 2 * P], U8, "w1w%d" % t) for t in range(PACK)]
        w1s = held([P, PACK, PASSES, P], U8, "w1s")

        def gather_half(h):
            piece = offs_sb[:, 32 * h : 32 * (h + 1)]
            for o in range(PASSES):
                nc.vector.tensor_copy(out=gs[h][:, o, :], in_=xs[:, T * o : T * (o + 1)].indirect(piece))
            for o in range(PASSES):
                nc.vector.tensor_copy(out=gw[h][o][:], in_=xw[:, T * o : T * (o + 1)].indirect(piece))

        def deal_w1(t):
            nc.vector.tensor_copy(
                out=w1w[t][:].rearrange("p o (m b) -> p o m b", b=2),
                in_=w1_raw[:].rearrange("p o (m t b) -> p o m t b", t=PACK, b=2)[:, :, :, t, :],
            )

        th = [held([P, PACK, HALF], F32, "th%d" % h) for h in range(HALVES)]
        mean = [held([P, PACK, HALF], F32, "mean%d" % h) for h in range(HALVES)]
        irt = [held([P, PACK, HALF], F32, "irt%d" % h) for h in range(HALVES)]
        num = [held([P, PACK, HALF], F32, "num%d" % h) for h in range(HALVES)]
        msum = held([P, PACK, V], F32, "msum")

        def mean_side(h):
            for t in range(PACK):
                mu = bank()
                for o in range(PASSES):
                    nc.tensor.matmul_mx(
                        out=mu[:],
                        lhsT=w1w[t][:, o, :].bitcast(FP4X4), lhsT_scale=w1s[:, t, o, :],
                        rhs=gw[h][o][:].bitcast(FP8X4), rhs_scale=gs[h][:, o, :],
                        start=(o == 0), stop=(o == PASSES - 1),
                    )
                nc.scalar.activation(
                    out=th[h][:, t, :].rearrange("p (d v) -> p d v", d=D),
                    in_=mu[:].rearrange("p (v d) -> p d v", d=D), func=ACT.Tanh,
                )
                nc.scalar.activation(out=mean[h][:, t, :], in_=th[h][:, t, :], func=ACT.Exp, scale=1.6)
                nc.scalar.activation(out=irt[h][:, t, :], in_=th[h][:, t, :], func=ACT.Exp, scale=-0.8)

        def by_member(ap):
            return ap.rearrange("p (d c i) -> p c d i", d=D, i=4)

        def by_entry(ap):
            return ap.rearrange("p (c i d) -> p c d i", d=D, i=4)

        for t in range(PACK):
            deal_w1(t)
        gs = [held([P, PASSES, HALF], U8, "gs0")]
        gather_half(0)
        for ts in (slice(0, 1), slice(1, PACK)):
            nc.vector.tensor_copy(
                out=w1s[:, ts].rearrange("p t o m -> p o t m"),
                in_=w1s_raw[:].rearrange("p (o m t) -> p o t m", o=PASSES, t=PACK)[:, :, ts, :],
            )
        gs.append(held([P, PASSES, HALF], U8, "gs1", "big_a1"))
        gather_half(1)

        loss_raw, exp_raw = [], []
        for h in range(HALVES):
            t_ = held([P, PACK, HALF], F32, "loss_raw%d" % h, ("w1_raw", "w1s_raw")[h])
            nc.sync.dma_start(out=t_[:], in_=loss.rearrange("(p t) j -> p t j", t=PACK)[:, :, HALF * h : HALF * (h + 1)])
            loss_raw.append(t_)
        w2w = held([P, PASSES, 2 * H], U8, "w2w", "xs")
        nc.sync.dma_start(out=w2w[:].bitcast(I32), in_=w2_words.rearrange("o p c -> p o c").bitcast(I32))
        mean_side(0)
        mean_side(1)

        dw = [[held([P, HALF], U32, "dw%d_%d" % (h, o), "w1w%d" % (2 * h + o)) for o in range(PASSES)] for h in range(HALVES)]
        dsc = held([P, HALVES, PASSES, HALF], U8, "dsc", "w1s")
        for h in range(HALVES):
            for o in range(PASSES):
                nc.vector.tensor_copy(out=by_member(dw[h][o][:].bitcast(I32)), in_=by_entry(gw[h][o][:].bitcast(I32)))
                nc.vector.tensor_copy(out=by_member(dsc[:, h, o, :]), in_=by_entry(gs[h][:, o, :]))

        w2s = load_scales(nc.gpsimd, w2_scales, "w2s", "gw0_0")
        for h in range(HALVES):
            t_ = held([P, PACK, HALF], F32, "exp_raw%d" % h, "gw%d_1" % h)
            nc.sync.dma_start(out=t_[:], in_=exp_.rearrange("(p t) j -> p t j", t=PACK)[:, :, HALF * h : HALF * (h + 1)])
            exp_raw.append(t_)
        unit_sb = held([P, PACK], F32, "unit_sb", "gs0")
        nc.sync.dma_start(out=unit_sb[:], in_=unit.rearrange("(p t) o -> p (t o)", t=PACK))
        neg_unit = held([P, PACK], F32, "neg_unit")
        nc.gpsimd.tensor_scalar(out=neg_unit[:], in0=unit_sb[:], scalar1=-1.0, scalar2=0.0, op0=ALU.mult, op1=ALU.add)
        w3w = held([P, 2 * N], U8, "w3w", "gw1_0")
        nc.sync.dma_start(out=w3w[:].bitcast(I32), in_=w3_words[0].bitcast(I32))
        w3s = load_scales(nc.gpsimd, w3_scales, "w3s", "big_a1")

        pair = [held([P, PACK, 2 * P], F32, "pair%d" % h) for h in range(HALVES)]
        for h in range(HALVES):
            nc.vector.tensor_tensor(out=pair[h][:], in0=mean[h][:, :, : 2 * P], in1=mean[h][:, :, 2 * P :], op=ALU.add)
            for t in range(PACK):
                nc.vector.tensor_tensor(
                    out=by_member(num[h][:, t, :]), in0=by_entry(loss_raw[h][:, t, :]), in1=by_member(mean[h][:, t, :]), op=ALU.add
                )
            nc.vector.tensor_tensor(
                out=msum[:, :, P * h : P * (h + 1)], in0=pair[h][:, :, :P], in1=pair[h][:, :, P:], op=ALU.add
            )
            nc.vector.scalar_tensor_tensor(
                out=num[h][:], in0=num[h][:], scalar=-0.5, in1=irt[h][:], op0=ALU.mult, op1=ALU.mult
            )

        ph = []
        sig = [held([P, D, H], F32, "sig%d" % h, ("w1_raw", "w1s_raw")[h]) for h in range(HALVES)]
        lg = held([P, HALVES * D, H], F32, "lg")
        for h in range(HALVES):
            for d in range(D):
                acc = bank()
                for o in range(PASSES):
                    nc.tensor.matmul_mx(
                        out=acc[:],
                        lhsT=dw[h][o][:, P * d : P * (d + 1)].bitcast(FP8X4), lhsT_scale=dsc[:, h, o, P * d : P * (d + 1)],
                        rhs=w2w[:, o, :].bitcast(FP4X4), rhs_scale=w2s[:, H * o : H * (o + 1)],
                        start=(o == 0), stop=(o == PASSES - 1),
                    )
                ph.append(acc)
                nc.scalar.activation(
                    out=sig[h][:, d, :].rearrange("p (t m) -> p t m", t=PACK),
                    in_=acc[:].rearrange("p (m t) -> p t m", t=PACK), func=ACT.Sigmoid, scale=-1.0,
                )
        for h in range(HALVES):
            for d in range(D):
                b = D * h + d
                nc.scalar.activation(out=lg[:, b, :], in_=sig[h][:, d, :], func=ACT.Ln, bias=TINY)
                nc.vector.scalar_tensor_tensor(
                    out=sig[h][:, d, :].rearrange("p (t m) -> p t m", t=PACK),
                    in0=lg[:, b, :].rearrange("p (t m) -> p t m", t=PACK), scalar=-1.0,
                    in1=ph[b][:].rearrange("p (m t) -> p t m", t=PACK), op0=ALU.mult, op1=ALU.max,
                )
        split = JOINT * P
        for h in range(HALVES):
            nc.scalar.activation(out=lg[:, D * h : D * (h + 1), split:], in_=sig[h][:, :, split:], func=ACT.Ln, bias=0.3)
        lm = held([P, PACK, V], F32, "lm")
        nc.scalar.activation(out=lm[:], in_=msum[:], func=ACT.Ln, scale=1.0 / 16.0)

        odd = held([P, HALVES, 2, split], F32, "odd", "th0")
        prod2 = held([P, HALVES, 2, split], F32, "prod2", "th1")
        prod4 = held([P, HALVES, split], F32, "prod4", "pair0")
        cof = held([P, HALVES, D, split], F32, "cof", "mean0")
        for h in range(HALVES):
            nc.vector.tensor_scalar(out=odd[:, h], in0=sig[h][:, 1::2, :split], scalar1=0.3, scalar2=None, op0=ALU.add)
        for h in range(HALVES):
            nc.vector.scalar_tensor_tensor(
                out=prod2[:, h], in0=sig[h][:, 0::2, :split], scalar=0.3, in1=odd[:, h], op0=ALU.add, op1=ALU.mult
            )
        nc.vector.tensor_tensor(out=prod4[:], in0=prod2[:, :, 0, :], in1=prod2[:, :, 1, :], op=ALU.mult)
        lp = held([P, HALVES, split], F32, "lp", "pair1")
        nc.scalar.activation(out=lp[:], in_=prod4[:], func=ACT.Ln)
        for h in range(HALVES):
            for a in range(2):
                nc.vector.tensor_tensor(out=cof[:, h, 2 * a, :], in0=odd[:, h, a, :], in1=prod2[:, h, 1 - a, :], op=ALU.mult)
                nc.vector.scalar_tensor_tensor(
                    out=cof[:, h, 2 * a + 1, :], in0=sig[h][:, 2 * a, :split], scalar=0.3, in1=prod2[:, h, 1 - a, :],
                    op0=ALU.add, op1=ALU.mult,
                )

        def deviance(t, h):
            acc = bank()
            for d in range(D):
                cols = slice(P * d, P * (d + 1))
                nc.tensor.matmul(out=acc[:, cols], lhsT=exp_raw[h][:, t, d::D], rhs=ident[:], is_transpose=True, start=True, stop=False)
                nc.tensor.matmul(out=acc[:, cols], lhsT=num[h][:, t, cols], rhs=ident[:], is_transpose=True, start=False, stop=True)
            return acc

        devi = {(t, h): deviance(t, h) for t in range(PACK) for h in range(HALVES)}

        late = held([P, PACK - JOINT + 1, HALVES * HALF], F32, "late", "pair0")
        fac = late[:, 0, :].rearrange("p (t v) -> p t v", t=PACK)
        rinv = {}
        for t in range(JOINT, PACK):
            rinv[t] = late[:, 1 + t - JOINT, :].rearrange("p (h d m) -> p h d m", h=HALVES, d=D)
            nc.scalar.activation(
                out=rinv[t].rearrange("p h d m -> p (h d) m"), in_=lg[:, :, P * t : P * (t + 1)], func=ACT.Exp, scale=-1.0
            )
        nc.scalar.activation(out=fac[:, JOINT:, :], in_=lm[:, JOINT:, :], func=ACT.Exp, scale=0.5)

        planes = held([P, PACK, U], BF16, "planes")
        wd = [held([P, HALVES, D, P], F32, "wd%d" % t, ("irt0", "irt1", "mean1", "wd3")[t]) for t in range(PACK)]

        def weigh(t, h):
            weight = cof[:, h, :, P * t : P * (t + 1)] if t < JOINT else rinv[t][:, h]
            nc.vector.tensor_tensor(
                out=wd[t][:, h], in0=devi[t, h][:].rearrange("p (d m) -> p d m", d=D), in1=weight, op=ALU.mult
            )

        def group_sums(t):
            grp = bank()
            for h in range(HALVES):
                for d in range(D):
                    nc.tensor.matmul(
                        out=grp[:, P * h : P * (h + 1)], lhsT=wd[t][:, h, d, :], rhs=ident[:],
                        is_transpose=True, start=(d == 0), stop=(d == D - 1),
                    )
            return grp

        weigh(0, 0)
        lpt = bank()
        for t in range(JOINT):
            for h in range(HALVES):
                nc.tensor.transpose(lpt[:, V * t + P * h : V * t + P * (h + 1)], lp[:, h, P * t : P * (t + 1)], ident[:])
        weigh(0, 1)
        joint = lm[:, :JOINT, :].rearrange("p t v -> p (t v)")
        nc.vector.scalar_tensor_tensor(
            out=joint, in0=lpt[:, : JOINT * V], scalar=-2.0, in1=joint, op0=ALU.mult, op1=ALU.add
        )
        nc.scalar.activation(out=fac[:, :JOINT, :], in_=lm[:, :JOINT, :], func=ACT.Exp, scale=0.5)
        vals = []
        for t in range(PACK):
            grp = group_sums(t)
            if t + 1 < PACK:
                weigh(t + 1, 0)
                weigh(t + 1, 1)
            val = held([P, V], F32, "val%d" % t)
            nc.vector.scalar_tensor_tensor(
                out=val[:], in0=grp[:, :V], scalar=neg_unit[:, t : t + 1], in1=fac[:, t, :], op0=ALU.mult, op1=ALU.mult
            )
            vals.append(val)

        for t in range(PACK):
            for q in range(U // PIECE):
                looked_up = vals[t][:].indirect(seg_sb[:, 8 * q : 8 * (q + 1)])
                dst = planes[:, t, PIECE * q : PIECE * (q + 1)]
                if t < PACK - 1:
                    nc.scalar.activation(out=dst, in_=looked_up, func=ACT.Copy)
                else:
                    nc.vector.tensor_copy(out=dst, in_=looked_up)

        for c in range(2):
            cols = slice(256 * c, 256 * (c + 1))
            hid = held([P, 256, PACK], BF16, "hid%d" % c)
            nc.vector.tensor_copy(
                out=hid[:].rearrange("p (c i) t -> p c t i", i=4),
                in_=planes[:, :, cols].rearrange("p t (c i) -> p c t i", i=4),
            )
            codes = held([P, 256], U32, "codes%d" % c)
            scales = held([P, 256], U8, "scales%d" % c)
            nc.vector.quantize_mx(out=codes[:].bitcast(FP8X4), scales=scales[:], in_=hid[:].rearrange("p r t -> p (r t)"))
            acc = bank()
            nc.tensor.matmul_mx(
                out=acc[:, :256], lhsT=w3w[:].bitcast(FP4X4), lhsT_scale=w3s[:],
                rhs=codes[:].bitcast(FP8X4), rhs_scale=scales[:], start=True, stop=True,
            )
            res = held([P, 256], F32, "res%d" % c)
            nc.scalar.copy(out=res[:], in_=acc[:, :256])
            nc.sync.dma_start(out=out[:, cols], in_=res[:])
